import numpy as np
import ml_dtypes


def mxq(x, axis, fmt="e4m3"):
    dtype, down = {"e4m3": (ml_dtypes.float8_e4m3fn, 7), "e5m2": (ml_dtypes.float8_e5m2, 14)}[fmt]
    v = np.moveaxis(np.asarray(x, np.float32).astype(ml_dtypes.bfloat16).astype(np.float64), axis, -1)
    blocks = v.reshape(v.shape[:-1] + (-1, 32))
    amax = np.abs(blocks).max(-1, keepdims=True)
    byte = np.maximum(np.where(amax > 0, np.frexp(amax)[1] - 1 + 127, 0) - down, 1)
    scale = np.exp2(byte - 127.0)
    codes = (blocks / scale).astype(np.float32).astype(dtype).astype(np.float64)
    return np.moveaxis((codes * scale).reshape(v.shape), -1, axis)


WIDE = False


def mx_kscale(k):
    if not WIDE:
        return np.ones(k)
    levels = np.array([10, -10, 5, -5, 0])
    if k % 512:
        return np.exp2(np.random.permutation(np.resize(levels, k // 32))).repeat(32)
    a = np.empty((k // 512, 16))
    for p in range(k // 512):
        a[p, :8] = np.random.permutation(np.resize(levels, 8))
        for g in range(8):
            far = levels[np.abs(levels - a[p, g]) >= 10]
            a[p, g + 8] = far[np.random.randint(len(far))]
    return np.exp2(a.ravel()).repeat(32)


def f64(x):
    return np.asarray(x).astype(np.float64)


def striped(idx):
    return np.tile(idx.reshape(-1, 16).T, (8, 1)).astype(np.uint16)


def unstriped(offs):
    return offs[:16].T.reshape(-1).astype(np.int64)


def striped8(idx):
    return np.concatenate([x.reshape(-1, 16).T for x in idx]).astype(np.uint16)


def runs(offs, k):
    lists = np.stack([offs[16 * r : 16 * r + 16].T.reshape(-1) for r in range(8)]).astype(np.int64)
    return lists[np.arange(k) % 512 // 64]


def pack_weight(w):
    k, n = w.shape
    w = f64(np.asarray(w, np.float32).astype(ml_dtypes.bfloat16)).reshape(k // 32, 32, n)
    amax = np.abs(w).max(1)
    byte = np.clip(np.where(amax > 0, np.frexp(amax)[1] - 1 + 127 - 7, 1), 1, 254)
    scaled = (w * np.exp2(127.0 - byte)[:, None, :]).reshape(k, n).astype(np.float32)
    words = np.ascontiguousarray(scaled.reshape(k // 512, 128, 4, n).transpose(0, 1, 3, 2)).astype(ml_dtypes.float8_e4m3fn).view(np.uint8)
    return words, np.ascontiguousarray(byte.astype(np.uint8).reshape(k // 512, 16, n))


def unpack_weight(words, scales):
    g, p, n, _ = words.shape
    vals = np.ascontiguousarray(words).view(ml_dtypes.float8_e4m3fn).astype(np.float64) * np.repeat(np.exp2(scales.astype(np.float64) - 127.0), 8, axis=1)[..., None]
    return vals.transpose(0, 1, 3, 2).reshape(g * 512, n)

def planes(y):
    n, m = y.shape
    v = y.astype(np.float32).astype(ml_dtypes.bfloat16).astype(np.float64).reshape(n // 32, 32, m)
    top = np.abs(v).max(1)
    byte = np.clip(np.where(top > 0, np.frexp(top)[1] - 1 + 127 - 7, 1), 1, 254)
    codes = (v * np.exp2(127.0 - byte)[:, None, :]).reshape(n, m).astype(np.float32).astype(ml_dtypes.float8_e4m3fn).view(np.uint8)
    words = codes.reshape(n // 512, 128, 4, m).transpose(0, 1, 3, 2)
    return np.ascontiguousarray(words), np.ascontiguousarray(byte.astype(np.uint8).reshape(n // 512, 16, m))


K, T, S, G, H, W, C = 512, 1024, 256, 2048, 512, 192, 512


def setup_inputs():
    n = np.random.standard_normal
    s = mx_kscale(K)[:, None]
    packed_xT = pack_weight(n((K, T)) * s)
    packed_dT = pack_weight(n((K, G)) / s)
    return {
        "x_words": packed_xT[0],
        "x_scales": packed_xT[1],
        "d_words": packed_dT[0],
        "d_scales": packed_dT[1],
        "gs": (np.random.uniform(0.5, 1.5, (K, 1)) / s).astype(np.float32),
        "offs": striped(np.random.permutation(T)[:S]),
        "k1": striped8(np.random.randint(0, G, (8, H))),
        "n1": striped(np.random.permutation(S)[:W]),
        "n2": striped(np.random.permutation(S)[:W]),
        "cand": striped(np.random.permutation(T)[:C]),
        "two": striped(np.random.permutation(T)[:S]),
        "k2": striped8(np.random.randint(0, G, (8, H))),
        "n3": striped8(np.stack([np.random.permutation(S) for _ in range(8)])),
        "n4": striped8(np.stack([np.random.permutation(S) for _ in range(8)])),
    }


def reference(x_words, x_scales, d_words, d_scales, gs, offs, k1, n1, n2, cand, two, k2, n3, n4):
    x_cand = unpack_weight(x_words, x_scales)[:, unstriped(cand)]
    d_k1 = unpack_weight(d_words, d_scales)[np.arange(K)[:, None], runs(k1, K)]
    xq = unpack_weight(x_words, x_scales)[:, unstriped(offs)]
    h = 0.0625 * (d_k1.T @ xq)
    old = h[:, unstriped(n1)]
    pa = h[:, unstriped(n2)]
    ra = old / (np.abs(pa) + 0.5)
    ds = h.copy()
    ds[:, unstriped(n1)] = ra
    z = f64(gs) * ds
    a = 0.0625 * ((x_cand.T @ mxq(z, 0, "e4m3")))
    d_k2 = unpack_weight(d_words, d_scales)[np.arange(K)[:, None], runs(k2, K)]
    x_two = unpack_weight(x_words, x_scales)[:, unstriped(two)]
    b = 0.0625 * (d_k2.T @ x_two)
    out_0 = np.maximum(a, b[np.arange(H)[:, None], runs(n4, H)]) - (np.minimum(a[np.arange(C)[:, None], runs(n3, C)], b))
    return (out_0,) + planes(out_0)

@@ -1,0 +1,210 @@
+from contextlib import ExitStack
+
+import concourse.mybir as mybir
+
+K, T, S, G, H, W, C = 512, 1024, 256, 2048, 512, 192, 512
+FLOPS = 2 * K * (H * S + C * S + H * S)
+
+F32 = mybir.dt.float32
+BF16 = mybir.dt.bfloat16
+I32 = mybir.dt.int32
+U32 = mybir.dt.uint32
+U16 = mybir.dt.uint16
+U8 = mybir.dt.uint8
+FP8X4 = mybir.dt.float8_e4m3fn_x4
+ALU = mybir.AluOpType
+ACT = mybir.ActivationFunctionType
+
+P = 128
+PACK = 4
+QUAD = 32
+SIXTEENTH = 0.0625
+WIDE = 2 * S
+
+
+def tile_picked_pqcjmaxbknorm_none_po_kernel(
+    tc, x_words, x_scales, d_words, d_scales, gs, offs, k1, n1, n2, cand, two, k2, n3, n4, out_0, out_1, out_2
+):
+    nc = tc.nc
+    with ExitStack() as ctx:
+        lists = ctx.enter_context(tc.tile_pool(name="lists", bufs=1))
+        sb = ctx.enter_context(tc.tile_pool(name="sb", bufs=1))
+        psum = ctx.enter_context(tc.psum_pool(name="psum", bufs=1))
+
+        def tile(name, shape, dtype, slot=None):
+            return sb.tile(shape, dtype, name=name, tag=slot or name, align_bytes=64)
+
+        def load_list(name, src):
+            held = lists.tile(list(src.shape), U16, name=name)
+            nc.sync.dma_start(held[:], src)
+            return held
+
+        def load_words(name, src):
+            held = tile(name, [P, src.shape[2]], I32)
+            nc.sync.dma_start(held[:], src[0].rearrange("p n r -> p (n r)").bitcast(I32))
+            return held
+
+        def load_scales(name, src):
+            held = tile(name, [P, src.shape[2]], U8)
+            words = src[0].bitcast(I32)
+            nc.sync.dma_start(held[:].bitcast(I32), words.unsqueeze(1).broadcast_to([words.shape[0], 8, words.shape[1]]))
+            return held
+
+        def deal(out, in_):
+            nc.vector.tensor_copy(out.rearrange("p (t m) -> p m t", t=PACK), in_.rearrange("p (m t) -> p m t", t=PACK))
+
+        def place_rows(engine, out, in_):
+            for q in range(P // QUAD):
+                engine.dma_start(out[QUAD * q : QUAD * q + 4, :].bitcast(I32), in_[QUAD * q : QUAD * (q + 1) : 8, :].bitcast(I32))
+
+        def pick_words(name, table, offsets, count, slot=None):
+            picked = tile(name, [P, count], I32, slot)
+            nc.vector.tensor_copy(picked[:].bitcast(U32), table[:].bitcast(U32).indirect(offsets[:]))
+            return picked
+
+        def pick_scales(name, table, offsets, count, slot=None):
+            picked = tile(name, [P, count], U8, slot)
+            nc.vector.tensor_copy(picked[:], table[:].indirect(offsets[:]))
+            return picked
+
+        def deal_words(name, picked):
+            dealt = tile(name, [P, H], I32)
+            deal(dealt[:], picked[:])
+            return dealt
+
+        def product(tag, rows, row_scales, t, cols, col_scales):
+            bank = psum.tile([P, S], F32, name=tag, tag=tag)
+            nc.tensor.matmul_mx(
+                bank[:],
+                lhsT=rows[:, P * t : P * (t + 1)].bitcast(FP8X4),
+                lhsT_scale=row_scales[:, P * t : P * (t + 1)],
+                rhs=cols.bitcast(FP8X4),
+                rhs_scale=col_scales,
+                start=True,
+                stop=True,
+            )
+            return bank
+
+        dsc = load_scales("dsc", d_scales)
+        k1_t = load_list("k1", k1)
+        xsc = load_scales("xsc", x_scales)
+        offs_t = load_list("offs", offs)
+        xw = load_words("xw", x_words)
+        dw = load_words("dw", d_words)
+        two_t = load_list("two", two)
+        k2_t = load_list("k2", k2)
+        cand_t = load_list("cand", cand)
+        n2_t = load_list("n2", n2)
+        n1_t = load_list("n1", n1)
+        n4_t = load_list("n4", n4)
+        n3_t = load_list("n3", n3)
+        gains = tile("gains", [P, PACK], F32)
+        nc.sync.dma_start(gains[:], gs.rearrange("(p t) o -> p (t o)", t=PACK))
+
+        h_scales = tile("h_scales", [P, H + S], U8)
+        nc.vector.memset(h_scales[:].bitcast(I32), 0)
+        late_scales = tile("late_scales", [P, H + C + S], U8)
+        nc.vector.memset(late_scales[:].bitcast(I32), 0)
+        z_scales = tile("z_scales", [P, S], U8)
+        nc.vector.memset(z_scales[:].bitcast(I32), 0)
+        half = tile("half", [P, 1], F32)
+        nc.vector.memset(half[:], 0.5)
+        a_win = [tile(f"a_win{t}", [P, WIDE], F32) for t in range(PACK)]
+        b_win = [tile(f"b_win{t}", [P, WIDE], F32) for t in range(PACK)]
+
+        h_dealt = tile("h_dealt", [P, H + S], U8)
+        k1_bytes = pick_scales("k1_bytes", dsc, k1_t, H)
+        offs_bytes = pick_scales("offs_bytes", xsc, offs_t, S)
+        deal(h_dealt[:, :H], k1_bytes[:])
+        nc.vector.tensor_copy(h_dealt[:, H:].bitcast(I32), offs_bytes[:].bitcast(I32))
+        place_rows(nc.scalar, h_scales, h_dealt)
+        xq = pick_words("xq", xw, offs_t, S)
+        late_dealt = tile("late_dealt", [P, H + C + S], U8)
+        two_bytes = pick_scales("two_bytes", xsc, two_t, S)
+        nc.vector.tensor_copy(late_dealt[:, H + C :].bitcast(I32), two_bytes[:].bitcast(I32))
+        d1 = deal_words("d1", pick_words("d1_picked", dw, k1_t, H))
+
+        deal(late_dealt[:, :H], pick_scales("k2_bytes", dsc, k2_t, H, "d1_picked")[:])
+
+        ds = [tile(f"ds{t}", [P, S], F32) for t in range(PACK)]
+        for t in range(PACK):
+            bank = product(f"bank{t}", d1, h_scales, t, xq[:], h_scales[:, H:])
+            if t < 2:
+                nc.scalar.activation(ds[t][:], bank[:], ACT.Copy, scale=SIXTEENTH)
+            else:
+                nc.vector.tensor_scalar(ds[t][:], bank[:], SIXTEENTH, None, ALU.mult)
+
+        old, root = [], []
+        for u in range(2):
+            pa = tile(f"pa{u}", [P, 2, W], F32)
+            size = tile(f"size{u}", [P, 2, W], F32)
+            old.append(tile(f"old{u}", [P, 2, W], F32))
+            root.append(tile(f"root{u}", [P, 2, W], F32))
+            for e in range(2):
+                nc.scalar.activation(pa[:, e, :], ds[2 * u + e][:].indirect(n2_t[:]), ACT.Copy)
+            nc.scalar.activation(old[u][:, 0, :], ds[2 * u][:].indirect(n1_t[:]), ACT.Copy)
+            nc.scalar.activation(size[:], pa[:], ACT.Abs)
+            nc.scalar.activation(old[u][:, 1, :], ds[2 * u + 1][:].indirect(n1_t[:]), ACT.Copy)
+            nc.scalar.activation(root[u][:], size[:], ACT.Abs_reciprocal_sqrt, bias=half[:])
+
+        cand_bytes = pick_scales("cand_bytes", xsc, cand_t, C, "d1")
+        once = [tile(f"once{u}", [P, 2, W], F32, ["xq", "d1"][u]) for u in range(2)]
+        ra = [tile(f"ra{u}", [P, 2, W], F32) for u in range(2)]
+        nc.vector.tensor_tensor(once[0][:], old[0][:], root[0][:], ALU.mult)
+        deal(late_dealt[:, H : H + C], cand_bytes[:])
+        place_rows(nc.sync, late_scales, late_dealt)
+        nc.vector.tensor_tensor(ra[0][:], once[0][:], root[0][:], ALU.mult)
+        d2_picked = pick_words("d2_picked", dw, k2_t, H, "old0")
+        nc.vector.tensor_tensor(once[1][:], old[1][:], root[1][:], ALU.mult)
+        d2 = deal_words("d2", d2_picked)
+        nc.vector.tensor_tensor(ra[1][:], once[1][:], root[1][:], ALU.mult)
+        for t in range(PACK):
+            nc.scalar.activation(ds[t][:].indirect(n1_t[:]), ra[t // 2][:, t % 2, :], ACT.Copy)
+
+        z_bf = tile("z_bf", [P, S, PACK], BF16)
+
+        def weigh(t):
+            nc.vector.tensor_scalar(z_bf[:, :, t], ds[t][:], gains[:, t : t + 1], None, ALU.mult)
+
+        x2 = pick_words("x2", xw, two_t, S, "d1")
+        weigh(0)
+        xc_picked = pick_words("xc_picked", xw, cand_t, C, "ds0")
+        weigh(1)
+        xc = deal_words("xc", xc_picked)
+        weigh(2)
+        weigh(3)
+        z_words = tile("z_words", [P, S], I32)
+        nc.vector.quantize_mx(z_words[:].bitcast(FP8X4), z_scales[:], z_bf[:].rearrange("p c t -> p (c t)"))
+
+        b_got = tile("b_got", [P, PACK, S], F32)
+        for t in range(PACK):
+            bank = product(f"bbank{t}", d2, late_scales, t, x2[:], late_scales[:, H + C :])
+            nc.scalar.activation(b_win[t][:, :S], bank[:], ACT.Copy, scale=SIXTEENTH)
+            nc.scalar.activation(b_got[:, t, :], b_win[t][:].indirect(n4_t[:]), ACT.Copy)
+
+        a_got = tile("a_got", [P, PACK, S], F32)
+        larger = tile("larger", [P, PACK, S], F32)
+        smaller = tile("smaller", [P, PACK, S], F32)
+        result = tile("result", [P, PACK, S], F32)
+        rows = out_0.rearrange("(p t) c -> p t c", t=PACK)
+        for t in range(PACK):
+            bank = product(f"bank{t}", xc, late_scales[:, H : H + C], t, z_words[:], z_scales[:])
+            nc.vector.tensor_scalar(a_win[t][:, :S], bank[:], SIXTEENTH, None, ALU.mult)
+            nc.scalar.activation(a_got[:, t, :], a_win[t][:].indirect(n3_t[:]), ACT.Copy)
+        for t in range(PACK):
+            nc.vector.tensor_tensor(larger[:, t, :], a_win[t][:, :S], b_got[:, t, :], ALU.max)
+        for t in range(PACK):
+            nc.vector.tensor_tensor(smaller[:, t, :], a_got[:, t, :], b_win[t][:, :S], ALU.min)
+            nc.vector.tensor_tensor(result[:, t, :], larger[:, t, :], smaller[:, t, :], ALU.subtract)
+            nc.sync.dma_start(rows[:, t, :], result[:, t, :])
+        out_bf = tile("out_bf", [P, S, PACK], BF16)
+        nc.vector.tensor_copy(
+            out_bf[:].rearrange("p (c i) t -> p c t i", i=4), result[:].rearrange("p t (c i) -> p c t i", i=4)
+        )
+        out_words = tile("out_words", [P, S], I32)
+        out_scales = tile("out_scales", [P, S], U8)
+        nc.vector.quantize_mx(out_words[:].bitcast(FP8X4), out_scales[:], out_bf[:].rearrange("p c t -> p (c t)"))
+        nc.sync.dma_start(out_1[0].rearrange("p c r -> p (c r)").bitcast(I32), out_words[:])
+        for q in range(P // QUAD):
+            engine = nc.scalar if q % 2 == 0 else nc.sync
+            engine.dma_start(out_2[0, 4 * q : 4 * q + 4, :].bitcast(I32), out_scales[QUAD * q : QUAD * q + 4, :].bitcast(I32))

@@ -29,6 +29,7 @@ def tile_picked_pqcjmaxbknorm_none_po_kernel(
     with ExitStack() as ctx:
         lists = ctx.enter_context(tc.tile_pool(name="lists", bufs=1))
         sb = ctx.enter_context(tc.tile_pool(name="sb", bufs=1))
+        shared = ctx.enter_context(tc.tile_pool(name="shared", bufs=1))
         psum = ctx.enter_context(tc.psum_pool(name="psum", bufs=1))
 
         def tile(name, shape, dtype, slot=None):
@@ -53,9 +54,9 @@ def tile_picked_pqcjmaxbknorm_none_po_kernel(
         def deal(out, in_):
             nc.vector.tensor_copy(out.rearrange("p (t m) -> p m t", t=PACK), in_.rearrange("p (m t) -> p m t", t=PACK))
 
-        def place_rows(engine, out, in_):
+        def place_rows(engine, out, in_, first=0):
             for q in range(P // QUAD):
-                engine.dma_start(out[QUAD * q : QUAD * q + 4, :].bitcast(I32), in_[QUAD * q : QUAD * (q + 1) : 8, :].bitcast(I32))
+                engine.dma_start(out[QUAD * q + first : QUAD * q + first + 4, :].bitcast(I32), in_[QUAD * q : QUAD * (q + 1) : 8, :].bitcast(I32))
 
         def pick_words(name, table, offsets, count, slot=None):
             picked = tile(name, [P, count], I32, slot)
@@ -85,101 +86,128 @@ def tile_picked_pqcjmaxbknorm_none_po_kernel(
             )
             return bank
 
-        dsc = load_scales("dsc", d_scales)
-        k1_t = load_list("k1", k1)
         xsc = load_scales("xsc", x_scales)
         offs_t = load_list("offs", offs)
-        xw = load_words("xw", x_words)
+        dsc = load_scales("dsc", d_scales)
+        k1_t = load_list("k1", k1)
         dw = load_words("dw", d_words)
+        xw = load_words("xw", x_words)
         two_t = load_list("two", two)
-        k2_t = load_list("k2", k2)
         cand_t = load_list("cand", cand)
+        k2_t = load_list("k2", k2)
         n2_t = load_list("n2", n2)
         n1_t = load_list("n1", n1)
-        n4_t = load_list("n4", n4)
-        n3_t = load_list("n3", n3)
         gains = tile("gains", [P, PACK], F32)
         nc.sync.dma_start(gains[:], gs.rearrange("(p t) o -> p (t o)", t=PACK))
+        n4_t = load_list("n4", n4)
+        n3_t = load_list("n3", n3)
 
-        h_scales = tile("h_scales", [P, H + S], U8)
-        nc.vector.memset(h_scales[:].bitcast(I32), 0)
-        late_scales = tile("late_scales", [P, H + C + S], U8)
-        nc.vector.memset(late_scales[:].bitcast(I32), 0)
-        z_scales = tile("z_scales", [P, S], U8)
-        nc.vector.memset(z_scales[:].bitcast(I32), 0)
         half = tile("half", [P, 1], F32)
         nc.vector.memset(half[:], 0.5)
+        warm = tile("warm", [P, 1], F32)
+        nc.scalar.activation(warm[:], half[:], ACT.Abs_reciprocal_sqrt)
+        early_scales = tile("early_scales", [P, H + S], U8)
+        late_placed = tile("late_placed", [P, H], U8)
+        x2_scales = tile("x2_scales", [P, S], U8)
+        z_scales = tile("z_scales", [P, S], U8)
+        for plane in (early_scales, late_placed, x2_scales, z_scales):
+            nc.vector.memset(plane[:].bitcast(I32), 0)
         a_win = [tile(f"a_win{t}", [P, WIDE], F32) for t in range(PACK)]
         b_win = [tile(f"b_win{t}", [P, WIDE], F32) for t in range(PACK)]
 
-        h_dealt = tile("h_dealt", [P, H + S], U8)
-        k1_bytes = pick_scales("k1_bytes", dsc, k1_t, H)
+        early_dealt = tile("early_dealt", [P, H + S], U8)
         offs_bytes = pick_scales("offs_bytes", xsc, offs_t, S)
-        deal(h_dealt[:, :H], k1_bytes[:])
-        nc.vector.tensor_copy(h_dealt[:, H:].bitcast(I32), offs_bytes[:].bitcast(I32))
-        place_rows(nc.scalar, h_scales, h_dealt)
+        k1_bytes = pick_scales("k1_bytes", dsc, k1_t, H)
+        nc.vector.tensor_copy(early_dealt[:, H:].bitcast(I32), offs_bytes[:].bitcast(I32))
+        deal(early_dealt[:, :H], k1_bytes[:])
+        place_rows(nc.scalar, early_scales, early_dealt)
+        d1_picked = pick_words("d1_picked", dw, k1_t, H)
+        d1 = shared.tile([P, H], I32, name="d1", offset=0, align_bytes=64)
+        deal(d1[:], d1_picked[:])
         xq = pick_words("xq", xw, offs_t, S)
-        late_dealt = tile("late_dealt", [P, H + C + S], U8)
-        two_bytes = pick_scales("two_bytes", xsc, two_t, S)
-        nc.vector.tensor_copy(late_dealt[:, H + C :].bitcast(I32), two_bytes[:].bitcast(I32))
-        d1 = deal_words("d1", pick_words("d1_picked", dw, k1_t, H))
-
-        deal(late_dealt[:, :H], pick_scales("k2_bytes", dsc, k2_t, H, "d1_picked")[:])
 
         ds = [tile(f"ds{t}", [P, S], F32) for t in range(PACK)]
         for t in range(PACK):
-            bank = product(f"bank{t}", d1, h_scales, t, xq[:], h_scales[:, H:])
+            bank = product(f"bank{t}", d1, early_scales, t, xq[:], early_scales[:, H:])
             if t < 2:
                 nc.scalar.activation(ds[t][:], bank[:], ACT.Copy, scale=SIXTEENTH)
             else:
                 nc.vector.tensor_scalar(ds[t][:], bank[:], SIXTEENTH, None, ALU.mult)
+        x2 = pick_words("x2", xw, two_t, S)
+        xc_picked = pick_words("xc_picked", xw, cand_t, C)
 
-        old, root = [], []
-        for u in range(2):
-            pa = tile(f"pa{u}", [P, 2, W], F32)
-            size = tile(f"size{u}", [P, 2, W], F32)
-            old.append(tile(f"old{u}", [P, 2, W], F32))
-            root.append(tile(f"root{u}", [P, 2, W], F32))
-            for e in range(2):
-                nc.scalar.activation(pa[:, e, :], ds[2 * u + e][:].indirect(n2_t[:]), ACT.Copy)
-            nc.scalar.activation(old[u][:, 0, :], ds[2 * u][:].indirect(n1_t[:]), ACT.Copy)
-            nc.scalar.activation(size[:], pa[:], ACT.Abs)
-            nc.scalar.activation(old[u][:, 1, :], ds[2 * u + 1][:].indirect(n1_t[:]), ACT.Copy)
-            nc.scalar.activation(root[u][:], size[:], ACT.Abs_reciprocal_sqrt, bias=half[:])
+        pa = [tile(f"pa{u}", [P, 2, W], F32) for u in range(2)]
+        size = [tile(f"size{u}", [P, 2, W], F32) for u in range(2)]
+        old = [tile(f"old{u}", [P, 2, W], F32) for u in range(2)]
+        root = [tile(f"root{u}", [P, 2, W], F32) for u in range(2)]
 
-        cand_bytes = pick_scales("cand_bytes", xsc, cand_t, C, "d1")
-        once = [tile(f"once{u}", [P, 2, W], F32, ["xq", "d1"][u]) for u in range(2)]
-        ra = [tile(f"ra{u}", [P, 2, W], F32) for u in range(2)]
-        nc.vector.tensor_tensor(once[0][:], old[0][:], root[0][:], ALU.mult)
-        deal(late_dealt[:, H : H + C], cand_bytes[:])
-        place_rows(nc.sync, late_scales, late_dealt)
-        nc.vector.tensor_tensor(ra[0][:], once[0][:], root[0][:], ALU.mult)
-        d2_picked = pick_words("d2_picked", dw, k2_t, H, "old0")
-        nc.vector.tensor_tensor(once[1][:], old[1][:], root[1][:], ALU.mult)
-        d2 = deal_words("d2", d2_picked)
-        nc.vector.tensor_tensor(ra[1][:], once[1][:], root[1][:], ALU.mult)
+        def look_up_h(into, t, offsets):
+            nc.scalar.activation(into[t // 2][:, t % 2, :], ds[t][:].indirect(offsets[:]), ACT.Copy)
+
+        def take_size(u):
+            nc.scalar.activation(size[u][:], pa[u][:], ACT.Abs)
+
+        def take_root(u):
+            nc.scalar.activation(root[u][:], size[u][:], ACT.Abs_reciprocal_sqrt, bias=half[:])
+
+        for t in range(3):
+            look_up_h(pa, t, n2_t)
+        take_size(0)
+        look_up_h(pa, 3, n2_t)
+        take_root(0)
+        look_up_h(old, 0, n1_t)
+        look_up_h(old, 1, n1_t)
+        take_size(1)
+        look_up_h(old, 2, n1_t)
+        take_root(1)
+        look_up_h(old, 3, n1_t)
+
+        def pick_late_scales(name, table, offsets, count, offset):
+            picked = shared.tile([P, count], U8, name=name, offset=offset, align_bytes=64)
+            nc.vector.tensor_copy(picked[:], table[:].indirect(offsets[:]))
+            return picked
+
+        place_rows(nc.sync, x2_scales, pick_late_scales("two_bytes", xsc, two_t, S, H + C))
+        place_rows(nc.sync, late_placed, pick_late_scales("k2_bytes", dsc, k2_t, H, 0))
+        place_rows(nc.sync, late_placed, pick_late_scales("cand_bytes", xsc, cand_t, C, H), 4)
+        once0 = tile("once0", [P, 2, W], F32)
+        ra = [tile("ra0", [P, 2, W], F32)]
+        nc.vector.tensor_tensor(once0[:], old[0][:], root[0][:], ALU.mult)
+        nc.vector.tensor_tensor(ra[0][:], once0[:], root[0][:], ALU.mult)
+        once1 = tile("once1", [P, 2, W], F32)
+        nc.vector.tensor_tensor(once1[:], old[1][:], root[1][:], ALU.mult)
+        late_scales = tile("late_scales", [P, H], U8, "root0")
+        deal(late_scales[:], late_placed[:])
+        ra.append(tile("ra1", [P, 2, W], F32, "late_placed"))
+        nc.vector.tensor_tensor(ra[1][:], once1[:], root[1][:], ALU.mult)
+        d2 = deal_words("d2", pick_words("d2_picked", dw, k2_t, H, "once1"))
+        xc = tile("xc", [P, C], I32, "once1")
+        deal(xc[:], xc_picked[:])
         for t in range(PACK):
             nc.scalar.activation(ds[t][:].indirect(n1_t[:]), ra[t // 2][:, t % 2, :], ACT.Copy)
 
-        z_bf = tile("z_bf", [P, S, PACK], BF16)
+        z_bf = tile("z_bf", [P, S, PACK], BF16, "root1")
 
         def weigh(t):
             nc.vector.tensor_scalar(z_bf[:, :, t], ds[t][:], gains[:, t : t + 1], None, ALU.mult)
 
-        x2 = pick_words("x2", xw, two_t, S, "d1")
+        def b_rows(t):
+            bank = product(f"bbank{t}", d2, late_scales, t, x2[:], x2_scales[:])
+            nc.vector.tensor_scalar(b_win[t][:, :S], bank[:], SIXTEENTH, None, ALU.mult)
+
         weigh(0)
-        xc_picked = pick_words("xc_picked", xw, cand_t, C, "ds0")
         weigh(1)
-        xc = deal_words("xc", xc_picked)
+        b_rows(0)
+        b_rows(1)
         weigh(2)
         weigh(3)
         z_words = tile("z_words", [P, S], I32)
         nc.vector.quantize_mx(z_words[:].bitcast(FP8X4), z_scales[:], z_bf[:].rearrange("p c t -> p (c t)"))
 
-        b_got = tile("b_got", [P, PACK, S], F32)
+        b_rows(2)
+        b_rows(3)
+        b_got = tile("b_got", [P, PACK, S], F32, "late_placed")
         for t in range(PACK):
-            bank = product(f"bbank{t}", d2, late_scales, t, x2[:], late_scales[:, H + C :])
-            nc.scalar.activation(b_win[t][:, :S], bank[:], ACT.Copy, scale=SIXTEENTH)
             nc.scalar.activation(b_got[:, t, :], b_win[t][:].indirect(n4_t[:]), ACT.Copy)
 
         a_got = tile("a_got", [P, PACK, S], F32)
@@ -187,23 +215,67 @@ def tile_picked_pqcjmaxbknorm_none_po_kernel(
         smaller = tile("smaller", [P, PACK, S], F32)
         result = tile("result", [P, PACK, S], F32)
         rows = out_0.rearrange("(p t) c -> p t c", t=PACK)
-        for t in range(PACK):
-            bank = product(f"bank{t}", xc, late_scales[:, H : H + C], t, z_words[:], z_scales[:])
-            nc.vector.tensor_scalar(a_win[t][:, :S], bank[:], SIXTEENTH, None, ALU.mult)
-            nc.scalar.activation(a_got[:, t, :], a_win[t][:].indirect(n3_t[:]), ACT.Copy)
-        for t in range(PACK):
-            nc.vector.tensor_tensor(larger[:, t, :], a_win[t][:, :S], b_got[:, t, :], ALU.max)
-        for t in range(PACK):
-            nc.vector.tensor_tensor(smaller[:, t, :], a_got[:, t, :], b_win[t][:, :S], ALU.min)
-            nc.vector.tensor_tensor(result[:, t, :], larger[:, t, :], smaller[:, t, :], ALU.subtract)
+        banks = [product(f"bank{t}", xc, late_scales[4:, :], t, z_words[:], z_scales[:]) for t in range(PACK)]
+
+        def take_larger(t):
+            nc.vector.scalar_tensor_tensor(larger[:, t, :], banks[t][:], SIXTEENTH, b_got[:, t, :], ALU.mult, ALU.max)
+
+        def leave_bank(t):
+            nc.scalar.activation(a_win[t][:, :S], banks[t][:], ACT.Copy, scale=SIXTEENTH)
+
+        def look_up_a(t, cols):
+            entries = n3_t[:, cols.start // 16 : cols.stop // 16]
+            nc.scalar.activation(a_got[:, t, cols], a_win[t][:].indirect(entries), ACT.Copy)
+
+        def take_smaller(t, cols):
+            nc.vector.tensor_tensor(smaller[:, t, cols], a_got[:, t, cols], b_win[t][:, cols], ALU.min)
+
+        def finish(t, cols):
+            nc.vector.tensor_tensor(result[:, t, cols], larger[:, t, cols], smaller[:, t, cols], ALU.subtract)
+
+        every = slice(0, S)
+        left, right = slice(0, S // 2), slice(S // 2, S)
+        last = PACK - 1
+        nc.vector.tensor_scalar(a_win[0][:, :S], banks[0][:], SIXTEENTH, None, ALU.mult)
+        for t in (1, 2, 3, 0):
+            take_larger(t)
+        look_up_a(0, every)
+        leave_bank(1)
+        leave_bank(2)
+        look_up_a(1, every)
+        leave_bank(3)
+        look_up_a(2, every)
+        look_up_a(last, left)
+        look_up_a(last, right)
+
+        for t in range(last):
+            take_smaller(t, every)
+            finish(t, every)
             nc.sync.dma_start(rows[:, t, :], result[:, t, :])
         out_bf = tile("out_bf", [P, S, PACK], BF16)
-        nc.vector.tensor_copy(
-            out_bf[:].rearrange("p (c i) t -> p c t i", i=4), result[:].rearrange("p t (c i) -> p c t i", i=4)
-        )
         out_words = tile("out_words", [P, S], I32)
         out_scales = tile("out_scales", [P, S], U8)
-        nc.vector.quantize_mx(out_words[:].bitcast(FP8X4), out_scales[:], out_bf[:].rearrange("p c t -> p (c t)"))
+
+        def rounded(cols):
+            return out_bf[:, cols, :].rearrange("p (c i) t -> p c t i", i=4)
+
+        def unrounded(cols):
+            return result[:, :, cols].rearrange("p t (c i) -> p c t i", i=4)
+
+        def quantize_out(cols):
+            nc.vector.quantize_mx(
+                out_words[:, cols].bitcast(FP8X4), out_scales[:, cols], out_bf[:, cols, :].rearrange("p c t -> p (c t)")
+            )
+
+        take_smaller(last, left)
+        finish(last, left)
+        nc.scalar.copy(rounded(left), unrounded(left))
+        take_smaller(last, right)
+        finish(last, right)
+        nc.sync.dma_start(rows[:, last, :], result[:, last, :])
+        nc.vector.tensor_copy(rounded(right), unrounded(right))
+        quantize_out(left)
+        quantize_out(right)
         nc.sync.dma_start(out_1[0].rearrange("p c r -> p (c r)").bitcast(I32), out_words[:])
         for q in range(P // QUAD):
             engine = nc.scalar if q % 2 == 0 else nc.sync

@@ -174,19 +174,21 @@ def tile_picked_pqcjmaxbknorm_none_po_kernel(
         ra = [tile("ra0", [P, 2, W], F32)]
         nc.vector.tensor_tensor(once0[:], old[0][:], root[0][:], ALU.mult)
         nc.vector.tensor_tensor(ra[0][:], once0[:], root[0][:], ALU.mult)
+        d2_picked = pick_words("d2_picked", dw, k2_t, H, "once0")
         once1 = tile("once1", [P, 2, W], F32)
         nc.vector.tensor_tensor(once1[:], old[1][:], root[1][:], ALU.mult)
         late_scales = tile("late_scales", [P, H], U8, "root0")
         deal(late_scales[:], late_placed[:])
         ra.append(tile("ra1", [P, 2, W], F32, "late_placed"))
         nc.vector.tensor_tensor(ra[1][:], once1[:], root[1][:], ALU.mult)
-        d2 = deal_words("d2", pick_words("d2_picked", dw, k2_t, H, "once1"))
-        xc = tile("xc", [P, C], I32, "once1")
+        d2 = tile("d2", [P, H], I32, "root1")
+        deal(d2[:], d2_picked[:])
+        xc = tile("xc", [P, C], I32, "once0")
         deal(xc[:], xc_picked[:])
         for t in range(PACK):
             nc.scalar.activation(ds[t][:].indirect(n1_t[:]), ra[t // 2][:, t % 2, :], ACT.Copy)
 
-        z_bf = tile("z_bf", [P, S, PACK], BF16, "root1")
+        z_bf = tile("z_bf", [P, S, PACK], BF16, "once1")
 
         def weigh(t):
             nc.vector.tensor_scalar(z_bf[:, :, t], ds[t][:], gains[:, t : t + 1], None, ALU.mult)
@@ -218,7 +220,7 @@ def tile_picked_pqcjmaxbknorm_none_po_kernel(
         banks = [product(f"bank{t}", xc, late_scales[4:, :], t, z_words[:], z_scales[:]) for t in range(PACK)]
 
         def take_larger(t):
-            nc.vector.scalar_tensor_tensor(larger[:, t, :], banks[t][:], SIXTEENTH, b_got[:, t, :], ALU.mult, ALU.max)
+            nc.vector.tensor_tensor(larger[:, t, :], a_win[t][:, :S], b_got[:, t, :], ALU.max)
 
         def leave_bank(t):
             nc.scalar.activation(a_win[t][:, :S], banks[t][:], ACT.Copy, scale=SIXTEENTH)
@@ -233,50 +235,50 @@ def tile_picked_pqcjmaxbknorm_none_po_kernel(
         def finish(t, cols):
             nc.vector.tensor_tensor(result[:, t, cols], larger[:, t, cols], smaller[:, t, cols], ALU.subtract)
 
+        def store(t):
+            nc.sync.dma_start(rows[:, t, :], result[:, t, :])
+
         every = slice(0, S)
         left, right = slice(0, S // 2), slice(S // 2, S)
         last = PACK - 1
-        nc.vector.tensor_scalar(a_win[0][:, :S], banks[0][:], SIXTEENTH, None, ALU.mult)
-        for t in (1, 2, 3, 0):
-            take_larger(t)
+        for t in range(2):
+            nc.vector.tensor_scalar(a_win[t][:, :S], banks[t][:], SIXTEENTH, None, ALU.mult)
         look_up_a(0, every)
-        leave_bank(1)
         leave_bank(2)
         look_up_a(1, every)
         leave_bank(3)
         look_up_a(2, every)
         look_up_a(last, left)
         look_up_a(last, right)
-
-        for t in range(last):
+        take_larger(0)
+        take_larger(1)
+        for t in range(2):
             take_smaller(t, every)
+            take_larger(t + 2)
             finish(t, every)
-            nc.sync.dma_start(rows[:, t, :], result[:, t, :])
+            store(t)
+        take_smaller(2, every)
+        take_smaller(last, left)
+        finish(2, every)
+        store(2)
+        take_smaller(last, right)
+        finish(last, left)
+        finish(last, right)
+        store(last)
+
         out_bf = tile("out_bf", [P, S, PACK], BF16)
         out_words = tile("out_words", [P, S], I32)
         out_scales = tile("out_scales", [P, S], U8)
-
-        def rounded(cols):
-            return out_bf[:, cols, :].rearrange("p (c i) t -> p c t i", i=4)
-
-        def unrounded(cols):
-            return result[:, :, cols].rearrange("p t (c i) -> p c t i", i=4)
-
-        def quantize_out(cols):
+        by_column = result[:].rearrange("p t c -> p c t")
+        nc.scalar.copy(out_bf[:, :, :2], by_column[:, :, :2])
+        for cols in (left, right):
+            nc.vector.tensor_copy(out_bf[:, cols, 2:], by_column[:, cols, 2:])
+        stored_words = out_1[0].rearrange("p c r -> p (c r)").bitcast(I32)
+        for cols in (left, right):
             nc.vector.quantize_mx(
                 out_words[:, cols].bitcast(FP8X4), out_scales[:, cols], out_bf[:, cols, :].rearrange("p c t -> p (c t)")
             )
-
-        take_smaller(last, left)
-        finish(last, left)
-        nc.scalar.copy(rounded(left), unrounded(left))
-        take_smaller(last, right)
-        finish(last, right)
-        nc.sync.dma_start(rows[:, last, :], result[:, last, :])
-        nc.vector.tensor_copy(rounded(right), unrounded(right))
-        quantize_out(left)
-        quantize_out(right)
-        nc.sync.dma_start(out_1[0].rearrange("p c r -> p (c r)").bitcast(I32), out_words[:])
+            nc.sync.dma_start(stored_words[:, cols], out_words[:, cols])
         for q in range(P // QUAD):
             engine = nc.scalar if q % 2 == 0 else nc.sync
             engine.dma_start(out_2[0, 4 * q : 4 * q + 4, :].bitcast(I32), out_scales[QUAD * q : QUAD * q + 4, :].bitcast(I32))

from contextlib import ExitStack

import concourse.mybir as mybir

K, T, S, G, H, W, C = 512, 1024, 256, 2048, 512, 192, 512
FLOPS = 2 * K * (H * S + C * S + H * S)

F32 = mybir.dt.float32
BF16 = mybir.dt.bfloat16
I32 = mybir.dt.int32
U32 = mybir.dt.uint32
U16 = mybir.dt.uint16
U8 = mybir.dt.uint8
FP8X4 = mybir.dt.float8_e4m3fn_x4
ALU = mybir.AluOpType
ACT = mybir.ActivationFunctionType

P = 128
PACK = 4
QUAD = 32
SIXTEENTH = 0.0625
WIDE = 2 * S


def tile_picked_pqcjmaxbknorm_none_po_kernel(
    tc, x_words, x_scales, d_words, d_scales, gs, offs, k1, n1, n2, cand, two, k2, n3, n4, out_0, out_1, out_2
):
    nc = tc.nc
    with ExitStack() as ctx:
        lists = ctx.enter_context(tc.tile_pool(name="lists", bufs=1))
        sb = ctx.enter_context(tc.tile_pool(name="sb", bufs=1))
        shared = ctx.enter_context(tc.tile_pool(name="shared", bufs=1))
        psum = ctx.enter_context(tc.psum_pool(name="psum", bufs=1))

        def tile(name, shape, dtype, slot=None):
            return sb.tile(shape, dtype, name=name, tag=slot or name, align_bytes=64)

        def load_list(name, src):
            held = lists.tile(list(src.shape), U16, name=name)
            nc.sync.dma_start(held[:], src)
            return held

        def load_words(name, src):
            held = tile(name, [P, src.shape[2]], I32)
            nc.sync.dma_start(held[:], src[0].rearrange("p n r -> p (n r)").bitcast(I32))
            return held

        def load_scales(name, src):
            held = tile(name, [P, src.shape[2]], U8)
            words = src[0].bitcast(I32)
            nc.sync.dma_start(held[:].bitcast(I32), words.unsqueeze(1).broadcast_to([words.shape[0], 8, words.shape[1]]))
            return held

        def deal(out, in_):
            nc.vector.tensor_copy(out.rearrange("p (t m) -> p m t", t=PACK), in_.rearrange("p (m t) -> p m t", t=PACK))

        def place_rows(engine, out, in_, first=0):
            for q in range(P // QUAD):
                engine.dma_start(out[QUAD * q + first : QUAD * q + first + 4, :].bitcast(I32), in_[QUAD * q : QUAD * (q + 1) : 8, :].bitcast(I32))

        def pick_words(name, table, offsets, count, slot=None):
            picked = tile(name, [P, count], I32, slot)
            nc.vector.tensor_copy(picked[:].bitcast(U32), table[:].bitcast(U32).indirect(offsets[:]))
            return picked

        def pick_scales(name, table, offsets, count, slot=None):
            picked = tile(name, [P, count], U8, slot)
            nc.vector.tensor_copy(picked[:], table[:].indirect(offsets[:]))
            return picked

        def deal_words(name, picked):
            dealt = tile(name, [P, H], I32)
            deal(dealt[:], picked[:])
            return dealt

        def product(tag, rows, row_scales, t, cols, col_scales):
            bank = psum.tile([P, S], F32, name=tag, tag=tag)
            nc.tensor.matmul_mx(
                bank[:],
                lhsT=rows[:, P * t : P * (t + 1)].bitcast(FP8X4),
                lhsT_scale=row_scales[:, P * t : P * (t + 1)],
                rhs=cols.bitcast(FP8X4),
                rhs_scale=col_scales,
                start=True,
                stop=True,
            )
            return bank

        xsc = load_scales("xsc", x_scales)
        offs_t = load_list("offs", offs)
        dsc = load_scales("dsc", d_scales)
        k1_t = load_list("k1", k1)
        dw = load_words("dw", d_words)
        xw = load_words("xw", x_words)
        two_t = load_list("two", two)
        cand_t = load_list("cand", cand)
        k2_t = load_list("k2", k2)
        n2_t = load_list("n2", n2)
        n1_t = load_list("n1", n1)
        gains = tile("gains", [P, PACK], F32)
        nc.sync.dma_start(gains[:], gs.rearrange("(p t) o -> p (t o)", t=PACK))
        n4_t = load_list("n4", n4)
        n3_t = load_list("n3", n3)

        half = tile("half", [P, 1], F32)
        nc.vector.memset(half[:], 0.5)
        warm = tile("warm", [P, 1], F32)
        nc.scalar.activation(warm[:], half[:], ACT.Abs_reciprocal_sqrt)
        early_scales = tile("early_scales", [P, H + S], U8)
        late_placed = tile("late_placed", [P, H], U8)
        x2_scales = tile("x2_scales", [P, S], U8)
        z_scales = tile("z_scales", [P, S], U8)
        for plane in (early_scales, late_placed, x2_scales, z_scales):
            nc.vector.memset(plane[:].bitcast(I32), 0)
        a_win = [tile(f"a_win{t}", [P, WIDE], F32) for t in range(PACK)]
        b_win = [tile(f"b_win{t}", [P, WIDE], F32) for t in range(PACK)]

        early_dealt = tile("early_dealt", [P, H + S], U8)
        offs_bytes = pick_scales("offs_bytes", xsc, offs_t, S)
        k1_bytes = pick_scales("k1_bytes", dsc, k1_t, H)
        nc.vector.tensor_copy(early_dealt[:, H:].bitcast(I32), offs_bytes[:].bitcast(I32))
        deal(early_dealt[:, :H], k1_bytes[:])
        place_rows(nc.scalar, early_scales, early_dealt)
        d1_picked = pick_words("d1_picked", dw, k1_t, H)
        d1 = shared.tile([P, H], I32, name="d1", offset=0, align_bytes=64)
        deal(d1[:], d1_picked[:])
        xq = pick_words("xq", xw, offs_t, S)

        ds = [tile(f"ds{t}", [P, S], F32) for t in range(PACK)]
        for t in range(PACK):
            bank = product(f"bank{t}", d1, early_scales, t, xq[:], early_scales[:, H:])
            if t < 2:
                nc.scalar.activation(ds[t][:], bank[:], ACT.Copy, scale=SIXTEENTH)
            else:
                nc.vector.tensor_scalar(ds[t][:], bank[:], SIXTEENTH, None, ALU.mult)
        x2 = pick_words("x2", xw, two_t, S)
        xc_picked = pick_words("xc_picked", xw, cand_t, C)

        pa = [tile(f"pa{u}", [P, 2, W], F32) for u in range(2)]
        size = [tile(f"size{u}", [P, 2, W], F32) for u in range(2)]
        old = [tile(f"old{u}", [P, 2, W], F32) for u in range(2)]
        root = [tile(f"root{u}", [P, 2, W], F32) for u in range(2)]

        def look_up_h(into, t, offsets):
            nc.scalar.activation(into[t // 2][:, t % 2, :], ds[t][:].indirect(offsets[:]), ACT.Copy)

        def take_size(u):
            nc.scalar.activation(size[u][:], pa[u][:], ACT.Abs)

        def take_root(u):
            nc.scalar.activation(root[u][:], size[u][:], ACT.Abs_reciprocal_sqrt, bias=half[:])

        for t in range(3):
            look_up_h(pa, t, n2_t)
        take_size(0)
        look_up_h(pa, 3, n2_t)
        take_root(0)
        look_up_h(old, 0, n1_t)
        look_up_h(old, 1, n1_t)
        take_size(1)
        look_up_h(old, 2, n1_t)
        take_root(1)
        look_up_h(old, 3, n1_t)

        def pick_late_scales(name, table, offsets, count, offset):
            picked = shared.tile([P, count], U8, name=name, offset=offset, align_bytes=64)
            nc.vector.tensor_copy(picked[:], table[:].indirect(offsets[:]))
            return picked

        place_rows(nc.sync, x2_scales, pick_late_scales("two_bytes", xsc, two_t, S, H + C))
        place_rows(nc.sync, late_placed, pick_late_scales("k2_bytes", dsc, k2_t, H, 0))
        place_rows(nc.sync, late_placed, pick_late_scales("cand_bytes", xsc, cand_t, C, H), 4)
        once0 = tile("once0", [P, 2, W], F32)
        ra = [tile("ra0", [P, 2, W], F32)]
        nc.vector.tensor_tensor(once0[:], old[0][:], root[0][:], ALU.mult)
        nc.vector.tensor_tensor(ra[0][:], once0[:], root[0][:], ALU.mult)
        d2_picked = pick_words("d2_picked", dw, k2_t, H, "once0")
        once1 = tile("once1", [P, 2, W], F32)
        nc.vector.tensor_tensor(once1[:], old[1][:], root[1][:], ALU.mult)
        late_scales = tile("late_scales", [P, H], U8, "root0")
        deal(late_scales[:], late_placed[:])
        ra.append(tile("ra1", [P, 2, W], F32, "late_placed"))
        nc.vector.tensor_tensor(ra[1][:], once1[:], root[1][:], ALU.mult)
        d2 = tile("d2", [P, H], I32, "root1")
        deal(d2[:], d2_picked[:])
        xc = tile("xc", [P, C], I32, "once0")
        deal(xc[:], xc_picked[:])
        for t in range(PACK):
            nc.scalar.activation(ds[t][:].indirect(n1_t[:]), ra[t // 2][:, t % 2, :], ACT.Copy)

        z_bf = tile("z_bf", [P, S, PACK], BF16, "once1")

        def weigh(t):
            nc.vector.tensor_scalar(z_bf[:, :, t], ds[t][:], gains[:, t : t + 1], None, ALU.mult)

        def b_rows(t):
            bank = product(f"bbank{t}", d2, late_scales, t, x2[:], x2_scales[:])
            nc.vector.tensor_scalar(b_win[t][:, :S], bank[:], SIXTEENTH, None, ALU.mult)

        weigh(0)
        weigh(1)
        b_rows(0)
        b_rows(1)
        weigh(2)
        weigh(3)
        z_words = tile("z_words", [P, S], I32)
        nc.vector.quantize_mx(z_words[:].bitcast(FP8X4), z_scales[:], z_bf[:].rearrange("p c t -> p (c t)"))

        b_rows(2)
        b_rows(3)
        b_got = tile("b_got", [P, PACK, S], F32, "late_placed")
        for t in range(PACK):
            nc.scalar.activation(b_got[:, t, :], b_win[t][:].indirect(n4_t[:]), ACT.Copy)

        a_got = tile("a_got", [P, PACK, S], F32)
        larger = tile("larger", [P, PACK, S], F32)
        smaller = tile("smaller", [P, PACK, S], F32)
        result = tile("result", [P, PACK, S], F32)
        rows = out_0.rearrange("(p t) c -> p t c", t=PACK)
        banks = [product(f"bank{t}", xc, late_scales[4:, :], t, z_words[:], z_scales[:]) for t in range(PACK)]

        def take_larger(t):
            nc.vector.tensor_tensor(larger[:, t, :], a_win[t][:, :S], b_got[:, t, :], ALU.max)

        def leave_bank(t):
            nc.scalar.activation(a_win[t][:, :S], banks[t][:], ACT.Copy, scale=SIXTEENTH)

        def look_up_a(t, cols):
            entries = n3_t[:, cols.start // 16 : cols.stop // 16]
            nc.scalar.activation(a_got[:, t, cols], a_win[t][:].indirect(entries), ACT.Copy)

        def take_smaller(t, cols):
            nc.vector.tensor_tensor(smaller[:, t, cols], a_got[:, t, cols], b_win[t][:, cols], ALU.min)

        def finish(t, cols):
            nc.vector.tensor_tensor(result[:, t, cols], larger[:, t, cols], smaller[:, t, cols], ALU.subtract)

        def store(t):
            nc.sync.dma_start(rows[:, t, :], result[:, t, :])

        every = slice(0, S)
        left, right = slice(0, S // 2), slice(S // 2, S)
        last = PACK - 1
        for t in range(2):
            nc.vector.tensor_scalar(a_win[t][:, :S], banks[t][:], SIXTEENTH, None, ALU.mult)
        look_up_a(0, every)
        leave_bank(2)
        look_up_a(1, every)
        leave_bank(3)
        look_up_a(2, every)
        look_up_a(last, left)
        look_up_a(last, right)
        take_larger(0)
        take_larger(1)
        for t in range(2):
            take_smaller(t, every)
            take_larger(t + 2)
            finish(t, every)
            store(t)
        take_smaller(2, every)
        take_smaller(last, left)
        finish(2, every)
        store(2)
        take_smaller(last, right)
        finish(last, left)
        finish(last, right)
        store(last)

        out_bf = tile("out_bf", [P, S, PACK], BF16)
        out_words = tile("out_words", [P, S], I32)
        out_scales = tile("out_scales", [P, S], U8)
        by_column = result[:].rearrange("p t c -> p c t")
        nc.scalar.copy(out_bf[:, :, :2], by_column[:, :, :2])
        for cols in (left, right):
            nc.vector.tensor_copy(out_bf[:, cols, 2:], by_column[:, cols, 2:])
        stored_words = out_1[0].rearrange("p c r -> p (c r)").bitcast(I32)
        for cols in (left, right):
            nc.vector.quantize_mx(
                out_words[:, cols].bitcast(FP8X4), out_scales[:, cols], out_bf[:, cols, :].rearrange("p c t -> p (c t)")
            )
            nc.sync.dma_start(stored_words[:, cols], out_words[:, cols])
        for q in range(P // QUAD):
            engine = nc.scalar if q % 2 == 0 else nc.sync
            engine.dma_start(out_2[0, 4 * q : 4 * q + 4, :].bitcast(I32), out_scales[QUAD * q : QUAD * q + 4, :].bitcast(I32))
